import numpy as np
import ml_dtypes


def mxq(x, axis, fmt="e4m3"):
    dtype, down = {"e4m3": (ml_dtypes.float8_e4m3fn, 7), "e5m2": (ml_dtypes.float8_e5m2, 14)}[fmt]
    v = np.moveaxis(np.asarray(x, np.float32).astype(ml_dtypes.bfloat16).astype(np.float64), axis, -1)
    blocks = v.reshape(v.shape[:-1] + (-1, 32))
    amax = np.abs(blocks).max(-1, keepdims=True)
    byte = np.maximum(np.where(amax > 0, np.frexp(amax)[1] - 1 + 127, 0) - down, 1)
    scale = np.exp2(byte - 127.0)
    codes = (blocks / scale).astype(np.float32).astype(dtype).astype(np.float64)
    return np.moveaxis((codes * scale).reshape(v.shape), -1, axis)


WIDE = False


def mx_kscale(k):
    if not WIDE:
        return np.ones(k)
    levels = np.array([10, -10, 5, -5, 0])
    if k % 512:
        return np.exp2(np.random.permutation(np.resize(levels, k // 32))).repeat(32)
    a = np.empty((k // 512, 16))
    for p in range(k // 512):
        a[p, :8] = np.random.permutation(np.resize(levels, 8))
        for g in range(8):
            far = levels[np.abs(levels - a[p, g]) >= 10]
            a[p, g + 8] = far[np.random.randint(len(far))]
    return np.exp2(a.ravel()).repeat(32)


BF16 = ml_dtypes.bfloat16


def bf(x):
    return np.asarray(x, np.float32).astype(BF16)


def f64(x):
    return np.asarray(x).astype(np.float64)


E2M1 = np.array([0.0, 0.5, 1.0, 1.5, 2.0, 3.0, 4.0, 6.0, -0.0, -0.5, -1.0, -1.5, -2.0, -3.0, -4.0, -6.0])


def pack_weight(w, fmt):
    k, n = w.shape
    w = f64(bf(w)).reshape(k // 32, 32, n)
    amax = np.abs(w).max(1)
    if fmt == "e4m3":
        byte = np.frexp(amax)[1] - 1 + 127 - 7
    else:
        mant, ex = np.frexp(amax / 6.0)
        byte = np.where(mant > 0.5, ex, ex - 1) + 127
    byte = np.clip(np.where(amax > 0, byte, 1), 1, 254)
    scaled = (w * np.exp2(127.0 - byte)[:, None, :]).reshape(k, n).astype(np.float32)
    by_word = np.ascontiguousarray(scaled.reshape(k // 512, 128, 4, n).transpose(0, 1, 3, 2))
    if fmt == "e4m3":
        words = by_word.astype(ml_dtypes.float8_e4m3fn).view(np.uint8)
    else:
        c = by_word.astype(ml_dtypes.float4_e2m1fn).view(np.uint8) & 0xF
        words = c[..., 0::2] | (c[..., 1::2] << 4)
    return np.ascontiguousarray(words), np.ascontiguousarray(byte.astype(np.uint8).reshape(k // 512, 16, n))


def unpack_weight(words, scales, fmt):
    g, p, n, _ = words.shape
    if fmt == "e4m3":
        vals = np.ascontiguousarray(words).view(ml_dtypes.float8_e4m3fn).astype(np.float64)
    else:
        nib = np.empty((g, p, n, 4), np.uint8)
        nib[..., 0::2] = words & 0xF
        nib[..., 1::2] = words >> 4
        vals = E2M1[nib]
    vals = vals * np.repeat(np.exp2(scales.astype(np.float64) - 127.0), 8, axis=1)[..., None]
    return vals.transpose(0, 1, 3, 2).reshape(g * 512, n)
def pack4(w):
    words, scales = pack_weight(w, "e2m1")
    return words.reshape(words.shape[0], 128, -1), scales


def unpack4(words, scales):
    return unpack_weight(words.reshape(words.shape[0], 128, -1, 2), scales, "e2m1")


def planes(Y):
    n, m = Y.shape
    b = f64(bf(Y)).reshape(n // 32, 32, m)
    amax = np.abs(b).max(1)
    byte = np.clip(np.where(amax > 0, np.frexp(amax)[1] - 1 + 127 - 7, 1), 1, 254)
    codes = (b * np.exp2(127.0 - byte)[:, None, :]).reshape(n, m).astype(np.float32).astype(ml_dtypes.float8_e4m3fn).view(np.uint8)
    words = codes.reshape(n // 512, 128, 4, m).transpose(0, 1, 3, 2)
    return np.ascontiguousarray(words), np.ascontiguousarray(byte.astype(np.uint8).reshape(n // 512, 16, m))


T, K, N = 1536, 2048, 512

GELU_A, GELU_B = np.sqrt(2.0 / np.pi), 0.044715

def setup_inputs():
    s = mx_kscale(K)[:, None]
    col = np.exp(0.7 * np.random.randn(N))
    x = np.random.randn(K, T)
    d = np.random.randn(K, N) / np.sqrt(K)
    v = np.random.randn(K, N) / np.sqrt(K) * col
    l = 0.7 * np.random.randn(K, N) / np.sqrt(K) * col
    r = 0.7 * np.random.randn(T, N) * col
    x_words, x_scales = pack_weight(x * s, "e4m3")
    v_words, v_scales = pack_weight(v / s, "e4m3")
    l_words, l_scales = pack4(l / s)
    return {"x_words": x_words, "x_scales": x_scales, "d": bf(d / s),
            "v_words": v_words, "v_scales": v_scales,
            "l_words": l_words, "l_scales": l_scales, "r": bf(r)}

def reference(x_words, x_scales, d, v_words, v_scales, l_words, l_scales, r):
    X = unpack_weight(x_words, x_scales, "e4m3").T
    V = unpack_weight(v_words, v_scales, "e4m3")
    L = unpack4(l_words, l_scales)
    D = mxq(f64(d), 0, "e4m3")
    u = X @ D
    gate = X @ V
    short = X @ L
    act = 0.5 * u * (1.0 + np.tanh(GELU_A * (u + GELU_B * u ** 3)))
    y = act * gate + short + f64(r)
    Y = y.T
    words, scales = planes(Y)
    return y, words, scales

@@ -1,0 +1,298 @@
+from contextlib import ExitStack
+
+import concourse.mybir as mybir
+from concourse.masks import make_identity
+
+T, K, N = 1536, 2048, 512
+FLOPS = 3 * 2 * T * K * N
+
+F32 = mybir.dt.float32
+BF16 = mybir.dt.bfloat16
+I32 = mybir.dt.int32
+U32 = mybir.dt.uint32
+U8 = mybir.dt.uint8
+FP8X4 = mybir.dt.float8_e4m3fn_x4
+FP4X4 = mybir.dt.float4_e2m1fn_x4
+ADD = mybir.AluOpType.add
+MULT = mybir.AluOpType.mult
+GELU = mybir.ActivationFunctionType.Gelu_apprx_tanh
+
+P = 128
+PASSES = K // 512
+TILES = T // P
+CHUNK_TILES = 6
+CHUNK = CHUNK_TILES * P
+BANKS = 8
+HALF = N // 2
+
+
+def tile_gated_adapter_bottleneck_k3_kernel(
+    tc, x_words, x_scales, d, v_words, v_scales, l_words, l_scales, r, out_0, out_1, out_2
+):
+    nc = tc.nc
+    with ExitStack() as ctx:
+        keep = ctx.enter_context(tc.tile_pool(name="keep", bufs=1))
+        work = ctx.enter_context(tc.tile_pool(name="work", bufs=4))
+        psum = ctx.enter_context(tc.psum_pool(name="psum", bufs=1))
+        ctx.enter_context(tc.manual_schedule())
+
+        def kept(name, shape, dtype):
+            return keep.tile(shape, dtype, name=name, align_bytes=256)
+
+        xw = [[kept("xw%d_%d" % (c, g), [P, CHUNK], U32) for g in range(PASSES)] for c in range(2)]
+        xs = [kept("xs%d" % c, [P, PASSES * CHUNK], U8) for c in range(2)]
+        lw = [kept("lw%d" % g, [P, 2 * N], U8) for g in range(PASSES)]
+        ls = kept("ls", [P, PASSES * N], U8)
+        vw = [kept("vw%d" % h, [P, 2, N], U32) for h in range(2)]
+        vs = kept("vs", [P, N], U8)
+        d_raw = [kept("d_raw%d" % g, [P, 4, N], BF16) for g in range(PASSES)]
+        d_grouped = [kept("d_grouped%d" % g, [P, N, 4], BF16) for g in range(PASSES)]
+        dw = [kept("dw%d" % g, [P, N], U32) for g in range(PASSES)]
+        ds = [kept("ds%d" % g, [P, N], U8) for g in range(PASSES)]
+        res = [kept("res%d" % c, [P, CHUNK_TILES, N], BF16) for c in range(2)]
+        short = [kept("short%d" % t, [P, N], F32) for t in range(CHUNK_TILES)]
+        short_res = [kept("short_res%d" % t, [P, N], F32) for t in range(CHUNK_TILES)]
+        y = [kept("y%d" % t, [P, N], F32) for t in range(TILES)]
+        y_bf = [kept("y_bf%d" % t, [P, N], BF16) for t in range(TILES)]
+        y_turned = kept("y_turned", [P, 4 * T], BF16)
+        y_codes = kept("y_codes", [P, T], U32)
+        y_scales = kept("y_scales", [P, T], U8)
+        ident = kept("ident", [P, P], F32)
+        warm = kept("warm", [P, 2], F32)
+
+        def bank(b):
+            return psum.tile([P, N], F32, name="bank%d" % b)
+
+        def load_x_words(queue, c, g):
+            rows = x_words[g].rearrange("p n t -> p (n t)")
+            queue.dma_start(out=xw[c][g][:].bitcast(I32), in_=rows[:, 4 * c * CHUNK : 4 * (c + 1) * CHUNK].bitcast(I32))
+
+        def load_l_words(queue, g):
+            queue.dma_start(out=lw[g][:].bitcast(I32), in_=l_words[g].bitcast(I32))
+
+        def load_scale_rows(queue, plane, rows, first, width):
+            by_row = rows.rearrange("g (q s) n -> s q g n", s=4)
+            for s in range(4):
+                queue.dma_start(
+                    out=plane[s:P:32, :].bitcast(I32).rearrange("q (g n) -> q g n", g=PASSES),
+                    in_=by_row[s][:, :, first : first + width].bitcast(I32),
+                )
+
+        def mx_pass(acc, t, g, which):
+            c, col = divmod(t, CHUNK_TILES)
+            cols = slice(col * P, (col + 1) * P)
+            x_scale = xs[c][:, g * CHUNK + col * P : g * CHUNK + (col + 1) * P]
+            if which == "short":
+                rhs, rhs_scale = lw[g][:].bitcast(FP4X4), ls[:, g * N : (g + 1) * N]
+            elif which == "gate":
+                rhs, rhs_scale = vw[g // 2][:, g % 2, :].bitcast(FP8X4), vs[4 * g :, :]
+            else:
+                rhs, rhs_scale = dw[g][:].bitcast(FP8X4), ds[g][:]
+            nc.tensor.matmul_mx(
+                out=acc[:], lhsT=xw[c][g][:, cols].bitcast(FP8X4), lhsT_scale=x_scale,
+                rhs=rhs, rhs_scale=rhs_scale, start=(g == 0), stop=(g == PASSES - 1),
+            )
+
+        def products(which, tiles, first_bank):
+            accs = {t: bank((first_bank + i) % BANKS) for i, t in enumerate(tiles)}
+            for g in range(PASSES):
+                for t in tiles:
+                    mx_pass(accs[t], t, g, which)
+            return accs
+
+        def quantize_d(g):
+            for engine_copy, lo in ((nc.vector.tensor_copy, 0), (nc.scalar.copy, HALF)):
+                engine_copy(
+                    out=d_grouped[g][:, lo : lo + HALF, :].rearrange("p (c i) t -> p c t i", i=4),
+                    in_=d_raw[g][:, :, lo : lo + HALF].rearrange("p t (c i) -> p c t i", i=4),
+                )
+            flat = d_grouped[g][:].rearrange("p n t -> p (n t)")
+            for lo in (0, HALF):
+                nc.vector.quantize_mx(
+                    out=dw[g][:, lo : lo + HALF].bitcast(FP8X4), scales=ds[g][:, lo : lo + HALF],
+                    in_=flat[:, 4 * lo : 4 * (lo + HALF)],
+                )
+
+        def residual(t):
+            return res[t // CHUNK_TILES][:, t % CHUNK_TILES, :]
+
+        def gelu(acc):
+            act = work.tile([P, N], F32, name="act")
+            nc.scalar.activation(out=act[:], in_=acc[:], func=GELU)
+            return act
+
+        def gated(act, acc):
+            prod = work.tile([P, N], F32, name="prod")
+            nc.vector.tensor_tensor(out=prod[:], in0=act[:], in1=acc[:], op=MULT)
+            return prod
+
+        def add(out, a, b):
+            nc.vector.tensor_tensor(out=out, in0=a, in1=b, op=ADD)
+
+        def by_pairs(ap):
+            return ap.rearrange("p (q u e) -> p u q e", u=2, e=2)
+
+        def pair_major(ap):
+            return ap.rearrange("p (u q e) -> p u q e", u=2, e=2)
+
+        def store_y(t):
+            nc.sync.dma_start(out=out_0[t * P : (t + 1) * P, :], in_=y[t][:])
+
+        def round_y(t):
+            nc.scalar.copy(out=pair_major(y_bf[t][:]), in_=by_pairs(y[t][:]))
+
+        def turn(tiles, b):
+            acc = bank(b % BANKS)
+            for i, t in enumerate(tiles):
+                words = y_bf[t][:].bitcast(F32)
+                for u in range(2):
+                    nc.tensor.transpose(acc[:, (2 * i + u) * P : (2 * i + u + 1) * P], words[:, u * P : (u + 1) * P], ident[:])
+            return acc
+
+        def copy_turned(tiles, acc):
+            lo, n = tiles[0] * P, len(tiles)
+            nc.scalar.copy(
+                out=y_turned[:, 4 * lo : 4 * (lo + n * P)].bitcast(F32).rearrange("p (a k u) -> p a k u", a=n, u=2),
+                in_=acc[:, : 2 * n * P].rearrange("p (a u k) -> p a k u", a=n, u=2),
+            )
+
+        def quantize_y(tiles):
+            lo, hi = tiles[0] * P, (tiles[-1] + 1) * P
+            nc.vector.quantize_mx(
+                out=y_codes[:, lo:hi].bitcast(FP8X4), scales=y_scales[:, lo:hi], in_=y_turned[:, 4 * lo : 4 * hi]
+            )
+
+        def store_codes(first, last):
+            rows = out_1[0].rearrange("p n t -> p (n t)")
+            nc.sync.dma_start(
+                out=rows[:, 4 * first * P : 4 * (last + 1) * P].bitcast(I32),
+                in_=y_codes[:, first * P : (last + 1) * P].bitcast(I32),
+            )
+
+        def store_scales(first, last, queues):
+            cols = slice(first * P, (last + 1) * P)
+            for q in range(4):
+                queues[q].dma_start(
+                    out=out_2[0][4 * q : 4 * q + 4, cols].bitcast(I32),
+                    in_=y_scales[32 * q : 32 * q + 4, cols].bitcast(I32),
+                )
+
+        nc.vector.memset(ls[:].bitcast(I32), 0)
+        nc.vector.memset(xs[0][:].bitcast(I32), 0)
+        load_x_words(nc.gpsimd, 0, 0)
+        load_l_words(nc.sync, 0)
+        load_scale_rows(nc.scalar, ls, l_scales, 0, N)
+        load_scale_rows(nc.sync, xs[0], x_scales, 0, CHUNK)
+        nc.vector.memset(vs[:].bitcast(I32), 0)
+        nc.vector.memset(xs[1][:].bitcast(I32), 0)
+        nc.vector.memset(warm[:], 0.0)
+        nc.scalar.activation(out=warm[:, 1:2], in_=warm[:, 0:1], func=GELU)
+        make_identity(nc, ident[:])
+        for g in range(1, PASSES):
+            load_l_words(nc.sync, g)
+            load_x_words(nc.sync, 0, g)
+        for q in range(4):
+            nc.sync.dma_start(
+                out=vs[32 * q : 32 * q + 16, :].bitcast(I32), in_=v_scales[:, 4 * q : 4 * q + 4, :].bitcast(I32)
+            )
+        for h in range(2):
+            nc.sync.dma_start(
+                out=vw[h][:].bitcast(I32),
+                in_=v_words[2 * h : 2 * h + 2].rearrange("g p n t -> p g (n t)").bitcast(I32),
+            )
+        for g in range(PASSES):
+            nc.sync.dma_start(out=d_raw[g][:], in_=d[512 * g : 512 * (g + 1), :].rearrange("(p j) n -> p j n", j=4))
+        nc.sync.dma_start(out=res[0][:], in_=r[:CHUNK, :].rearrange("(a p) n -> p a n", p=P))
+        load_scale_rows(nc.sync, xs[1], x_scales, CHUNK, CHUNK)
+        for g in range(PASSES):
+            load_x_words(nc.sync, 1, g)
+        nc.sync.dma_start(out=res[1][:], in_=r[CHUNK:, :].rearrange("(a p) n -> p a n", p=P))
+
+        s_acc = products("short", range(CHUNK_TILES), 0)
+        for t in range(CHUNK_TILES):
+            engine_copy = nc.vector.tensor_copy if t % 2 == 0 else nc.scalar.copy
+            engine_copy(out=short[t][:], in_=s_acc[t][:])
+        g_acc = products("gate", (0, 1), 6)
+        g_acc.update(products("gate", (2, 3), 0))
+        for g in range(PASSES):
+            quantize_d(g)
+        u_acc = products("down", range(4), 2)
+        for t in range(4):
+            add(short_res[t][:], short[t][:], residual(t))
+        acts = {t: gelu(u_acc[t]) for t in range(4)}
+        ring = 2
+        prods = {}
+
+        def finish_head(t):
+            add(y[t][:], prods[t][:], short_res[t][:])
+            store_y(t)
+            round_y(t)
+
+        u_acc.update(products("down", (4,), 2))
+        g_acc.update(products("gate", (4,), 3))
+        u_acc.update(products("down", (5,), 4))
+        g_acc.update(products("gate", (5,), 5))
+        ring = 6
+        prods[0] = gated(acts[0], g_acc[0])
+        acts[4] = gelu(u_acc[4])
+        prods[1] = gated(acts[1], g_acc[1])
+        finish_head(0)
+        prods[2] = gated(acts[2], g_acc[2])
+        finish_head(1)
+        acts[5] = gelu(u_acc[5])
+        prods[3] = gated(acts[3], g_acc[3])
+        finish_head(2)
+        add(short_res[4][:], short[4][:], residual(4))
+        finish_head(3)
+        add(short_res[5][:], short[5][:], residual(5))
+        prods[4] = gated(acts[4], g_acc[4])
+        prods[5] = gated(acts[5], g_acc[5])
+
+        turn_after = {6: [(0, 1), (2, 3)], 10: [(4, 5), (6, 7), (8, 9)]}
+        for t in range(CHUNK_TILES, TILES - 1):
+            act = gelu(products("down", (t,), ring)[t])
+            if t == CHUNK_TILES:
+                finish_head(4)
+                finish_head(5)
+            prod = gated(act, products("gate", (t,), ring + 1)[t])
+            prod_res = work.tile([P, N], F32, name="prod_res")
+            add(prod_res[:], prod[:], residual(t))
+            acc = products("short", (t,), ring + 2)[t]
+            ring += 3
+            pairs = turn_after.get(t, [])
+            for pair in pairs:
+                copy_turned(pair, turn(pair, ring))
+                ring += 1
+            add(y[t][:], prod_res[:], acc[:])
+            store_y(t)
+            round_y(t)
+            for pair in pairs:
+                quantize_y(pair)
+            if pairs:
+                store_codes(pairs[0][0], pairs[-1][1])
+        store_scales(0, TILES - 3, [nc.sync] * 4)
+
+        t = TILES - 1
+        act = gelu(products("down", (t,), ring)[t])
+        acc = products("gate", (t,), ring + 1)[t]
+        prod = work.tile([P, N], F32, name="prod")
+        prod_res = work.tile([P, N], F32, name="prod_res")
+        halves = (slice(0, HALF), slice(HALF, N))
+        for cols in halves:
+            nc.vector.tensor_tensor(out=prod[:, cols], in0=act[:, cols], in1=acc[:, cols], op=MULT)
+        for cols in halves:
+            add(prod_res[:, cols], prod[:, cols], residual(t)[:, cols])
+        acc = products("short", (t,), ring + 2)[t]
+        copy_turned((t - 1,), turn((t - 1,), ring + 3))
+        add(y_bf[t][:], prod_res[:], acc[:])
+        add(y[t][:], prod_res[:], acc[:])
+        store_y(t)
+        last = bank((ring + 4) % BANKS)
+        words = y_bf[t][:].bitcast(F32)
+        for u in range(2):
+            nc.tensor.transpose(last[:, u * P : (u + 1) * P], words[:, u : 2 * P : 2], ident[:])
+        copy_turned((t,), last)
+        quantize_y((t - 1,))
+        quantize_y((t,))
+        store_codes(t - 1, t)
+        store_scales(t - 1, t, [nc.scalar, nc.scalar, nc.sync, nc.sync])

@@ -217,7 +217,7 @@ def tile_gated_adapter_bottleneck_k3_kernel(
         for g in range(PASSES):
             quantize_d(g)
         u_acc = products("down", range(4), 2)
-        for t in range(4):
+        for t in range(CHUNK_TILES):
             add(short_res[t][:], short[t][:], residual(t))
         acts = {t: gelu(u_acc[t]) for t in range(4)}
         ring = 2
@@ -242,57 +242,66 @@ def tile_gated_adapter_bottleneck_k3_kernel(
         acts[5] = gelu(u_acc[5])
         prods[3] = gated(acts[3], g_acc[3])
         finish_head(2)
-        add(short_res[4][:], short[4][:], residual(4))
         finish_head(3)
-        add(short_res[5][:], short[5][:], residual(5))
         prods[4] = gated(acts[4], g_acc[4])
         prods[5] = gated(acts[5], g_acc[5])
 
-        turn_after = {6: [(0, 1), (2, 3)], 10: [(4, 5), (6, 7), (8, 9)]}
+        early_pairs = [(0, 1), (2, 3), (4, 5), (6, 7)]
+        turned = []
+
+        def finish_pairs(pairs):
+            for pair in pairs:
+                copy_turned(pair, turned.pop(0))
+
         for t in range(CHUNK_TILES, TILES - 1):
             act = gelu(products("down", (t,), ring)[t])
             if t == CHUNK_TILES:
                 finish_head(4)
                 finish_head(5)
+            else:
+                round_y(t - 1)
+            if t == 9:
+                finish_pairs(early_pairs[2:])
             prod = gated(act, products("gate", (t,), ring + 1)[t])
+            if t == 9:
+                quantize_y(early_pairs[0])
+                quantize_y(early_pairs[1])
+            if t == 10:
+                quantize_y(early_pairs[2])
+                quantize_y(early_pairs[3])
+                store_codes(0, 7)
+                store_scales(0, 7, [nc.sync] * 4)
             prod_res = work.tile([P, N], F32, name="prod_res")
             add(prod_res[:], prod[:], residual(t))
             acc = products("short", (t,), ring + 2)[t]
             ring += 3
-            pairs = turn_after.get(t, [])
-            for pair in pairs:
-                copy_turned(pair, turn(pair, ring))
-                ring += 1
+            if t == 8:
+                for pair in early_pairs:
+                    turned.append(turn(pair, ring))
+                    ring += 1
+                finish_pairs(early_pairs[:2])
             add(y[t][:], prod_res[:], acc[:])
             store_y(t)
-            round_y(t)
-            for pair in pairs:
-                quantize_y(pair)
-            if pairs:
-                store_codes(pairs[0][0], pairs[-1][1])
-        store_scales(0, TILES - 3, [nc.sync] * 4)
 
         t = TILES - 1
         act = gelu(products("down", (t,), ring)[t])
-        acc = products("gate", (t,), ring + 1)[t]
-        prod = work.tile([P, N], F32, name="prod")
+        round_y(t - 1)
+        prod = gated(act, products("gate", (t,), ring + 1)[t])
         prod_res = work.tile([P, N], F32, name="prod_res")
-        halves = (slice(0, HALF), slice(HALF, N))
-        for cols in halves:
-            nc.vector.tensor_tensor(out=prod[:, cols], in0=act[:, cols], in1=acc[:, cols], op=MULT)
-        for cols in halves:
-            add(prod_res[:, cols], prod[:, cols], residual(t)[:, cols])
-        acc = products("short", (t,), ring + 2)[t]
-        copy_turned((t - 1,), turn((t - 1,), ring + 3))
+        add(prod_res[:], prod[:], residual(t))
+        for i, tiles in enumerate(((8, 9), (10,))):
+            copy_turned(tiles, turn(tiles, ring + 2 + i))
+            quantize_y(tiles)
+        store_codes(8, 10)
+        acc = products("short", (t,), ring + 4)[t]
         add(y_bf[t][:], prod_res[:], acc[:])
         add(y[t][:], prod_res[:], acc[:])
         store_y(t)
-        last = bank((ring + 4) % BANKS)
+        last = bank((ring + 5) % BANKS)
         words = y_bf[t][:].bitcast(F32)
         for u in range(2):
             nc.tensor.transpose(last[:, u * P : (u + 1) * P], words[:, u : 2 * P : 2], ident[:])
         copy_turned((t,), last)
-        quantize_y((t - 1,))
         quantize_y((t,))
-        store_codes(t - 1, t)
-        store_scales(t - 1, t, [nc.scalar, nc.scalar, nc.sync, nc.sync])
+        store_codes(t, t)
+        store_scales(8, t, [nc.scalar, nc.scalar, nc.sync, nc.sync])

@@ -24,6 +24,7 @@ CHUNK_TILES = 6
 CHUNK = CHUNK_TILES * P
 BANKS = 8
 HALF = N // 2
+WARM_PASSES = 20
 
 
 def tile_gated_adapter_bottleneck_k3_kernel(
@@ -58,6 +59,9 @@ def tile_gated_adapter_bottleneck_k3_kernel(
         y_codes = kept("y_codes", [P, T], U32)
         y_scales = kept("y_scales", [P, T], U8)
         ident = kept("ident", [P, P], F32)
+        zero = kept("zero", [P, 4 * P], BF16)
+        zero_codes = kept("zero_codes", [P, P], U32)
+        zero_scales = kept("zero_scales", [P, P], U8)
         warm = kept("warm", [P, 2], F32)
 
         def bank(b):
@@ -70,26 +74,26 @@ def tile_gated_adapter_bottleneck_k3_kernel(
         def load_l_words(queue, g):
             queue.dma_start(out=lw[g][:].bitcast(I32), in_=l_words[g].bitcast(I32))
 
-        def load_scale_rows(queue, plane, rows, first, width):
+        def load_scale_rows(queue, plane, rows, first, width, which=range(4)):
             by_row = rows.rearrange("g (q s) n -> s q g n", s=4)
-            for s in range(4):
+            for s in which:
                 queue.dma_start(
                     out=plane[s:P:32, :].bitcast(I32).rearrange("q (g n) -> q g n", g=PASSES),
                     in_=by_row[s][:, :, first : first + width].bitcast(I32),
                 )
 
-        def mx_pass(acc, t, g, which):
+        def mx_pass(acc, t, g, which, lo=0, hi=N):
             c, col = divmod(t, CHUNK_TILES)
             cols = slice(col * P, (col + 1) * P)
             x_scale = xs[c][:, g * CHUNK + col * P : g * CHUNK + (col + 1) * P]
             if which == "short":
-                rhs, rhs_scale = lw[g][:].bitcast(FP4X4), ls[:, g * N : (g + 1) * N]
+                rhs, rhs_scale = lw[g][:, 2 * lo : 2 * hi].bitcast(FP4X4), ls[:, g * N + lo : g * N + hi]
             elif which == "gate":
                 rhs, rhs_scale = vw[g // 2][:, g % 2, :].bitcast(FP8X4), vs[4 * g :, :]
             else:
                 rhs, rhs_scale = dw[g][:].bitcast(FP8X4), ds[g][:]
             nc.tensor.matmul_mx(
-                out=acc[:], lhsT=xw[c][g][:, cols].bitcast(FP8X4), lhsT_scale=x_scale,
+                out=acc[:, : hi - lo], lhsT=xw[c][g][:, cols].bitcast(FP8X4), lhsT_scale=x_scale,
                 rhs=rhs, rhs_scale=rhs_scale, start=(g == 0), stop=(g == PASSES - 1),
             )
 
@@ -178,11 +182,20 @@ def tile_gated_adapter_bottleneck_k3_kernel(
                 )
 
         nc.vector.memset(ls[:].bitcast(I32), 0)
+        nc.vector.memset(zero[:], 0.0)
         nc.vector.memset(xs[0][:].bitcast(I32), 0)
-        load_x_words(nc.gpsimd, 0, 0)
         load_l_words(nc.sync, 0)
-        load_scale_rows(nc.scalar, ls, l_scales, 0, N)
-        load_scale_rows(nc.sync, xs[0], x_scales, 0, CHUNK)
+        load_scale_rows(nc.sync, ls, l_scales, 0, N)
+        load_scale_rows(nc.sync, xs[0], x_scales, 0, CHUNK, (0, 1))
+        load_x_words(nc.sync, 0, 0)
+        load_scale_rows(nc.sync, xs[0], x_scales, 0, CHUNK, (2, 3))
+        nc.vector.quantize_mx(out=zero_codes[:].bitcast(FP8X4), scales=zero_scales[:], in_=zero[:])
+        idle = bank(BANKS - 1)
+        for i in range(WARM_PASSES):
+            nc.tensor.matmul_mx(
+                out=idle[:, (i % 4) * P : (i % 4 + 1) * P], lhsT=zero_codes[:].bitcast(FP8X4), lhsT_scale=zero_scales[:],
+                rhs=zero_codes[:].bitcast(FP8X4), rhs_scale=zero_scales[:], start=True, stop=True,
+            )
         nc.vector.memset(vs[:].bitcast(I32), 0)
         nc.vector.memset(xs[1][:].bitcast(I32), 0)
         nc.vector.memset(warm[:], 0.0)
@@ -293,11 +306,18 @@ def tile_gated_adapter_bottleneck_k3_kernel(
             copy_turned(tiles, turn(tiles, ring + 2 + i))
             quantize_y(tiles)
         store_codes(8, 10)
-        acc = products("short", (t,), ring + 4)[t]
-        add(y_bf[t][:], prod_res[:], acc[:])
-        add(y[t][:], prod_res[:], acc[:])
+        quarters = []
+        for i in range(4):
+            acc = bank((ring + 4 + i) % BANKS)
+            for g in range(PASSES):
+                mx_pass(acc, t, g, "short", i * P, (i + 1) * P)
+            cols = slice(i * P, (i + 1) * P)
+            add(y_bf[t][:, cols], prod_res[:, cols], acc[:, :P])
+            quarters.append((cols, acc))
+        for cols, acc in quarters:
+            add(y[t][:, cols], prod_res[:, cols], acc[:, :P])
         store_y(t)
-        last = bank((ring + 5) % BANKS)
+        last = bank((ring + 8) % BANKS)
         words = y_bf[t][:].bitcast(F32)
         for u in range(2):
             nc.tensor.transpose(last[:, u * P : (u + 1) * P], words[:, u : 2 * P : 2], ident[:])

@@ -24,7 +24,9 @@ CHUNK_TILES = 6
 CHUNK = CHUNK_TILES * P
 BANKS = 8
 HALF = N // 2
-WARM_PASSES = 20
+WARM_PASSES = 16
+BLOCK_TILES = 9
+FIRST = CHUNK // 2
 
 
 def tile_gated_adapter_bottleneck_k3_kernel(
@@ -41,23 +43,28 @@ def tile_gated_adapter_bottleneck_k3_kernel(
             return keep.tile(shape, dtype, name=name, align_bytes=256)
 
         xw = [[kept("xw%d_%d" % (c, g), [P, CHUNK], U32) for g in range(PASSES)] for c in range(2)]
+        xp = kept("xp", [P, CHUNK], U8)
         xs = [kept("xs%d" % c, [P, PASSES * CHUNK], U8) for c in range(2)]
-        lw = [kept("lw%d" % g, [P, 2 * N], U8) for g in range(PASSES)]
+        lw = [kept("lw%d" % h, [P, 2, 2 * N], U8) for h in range(2)]
         ls = kept("ls", [P, PASSES * N], U8)
-        vw = [kept("vw%d" % h, [P, 2, N], U32) for h in range(2)]
+        vw = [kept("vw%d" % g, [P, N], U32) for g in range(PASSES)]
         vs = kept("vs", [P, N], U8)
         d_raw = [kept("d_raw%d" % g, [P, 4, N], BF16) for g in range(PASSES)]
         d_grouped = [kept("d_grouped%d" % g, [P, N, 4], BF16) for g in range(PASSES)]
         dw = [kept("dw%d" % g, [P, N], U32) for g in range(PASSES)]
         ds = [kept("ds%d" % g, [P, N], U8) for g in range(PASSES)]
         res = [kept("res%d" % c, [P, CHUNK_TILES, N], BF16) for c in range(2)]
-        short = [kept("short%d" % t, [P, N], F32) for t in range(CHUNK_TILES)]
+        gate = [kept("gate%d" % t, [P, N], F32) for t in range(CHUNK_TILES)]
         short_res = [kept("short_res%d" % t, [P, N], F32) for t in range(CHUNK_TILES)]
-        y = [kept("y%d" % t, [P, N], F32) for t in range(TILES)]
+        y_pairs = [kept("y%d" % k, [P, 2, N], F32) for k in range(TILES // 2)]
+        y = [y_pairs[t // 2][:, t % 2, :] for t in range(TILES)]
         y_bf = [kept("y_bf%d" % t, [P, N], BF16) for t in range(TILES)]
-        y_turned = kept("y_turned", [P, 4 * T], BF16)
-        y_codes = kept("y_codes", [P, T], U32)
-        y_scales = kept("y_scales", [P, T], U8)
+        late = TILES - BLOCK_TILES
+        y_turned = kept("y_turned", [P, 4 * late * P], BF16)
+        y_codes = kept("y_codes", [P, late * P], U32)
+        y_scales = kept("y_scales", [P, late * P], U8)
+        block_codes = kept("block_codes", [P, BLOCK_TILES * P], U32)
+        block_scales = kept("block_scales", [P, BLOCK_TILES * P], U8)
         ident = kept("ident", [P, P], F32)
         zero = kept("zero", [P, 4 * P], BF16)
         zero_codes = kept("zero_codes", [P, P], U32)
@@ -67,12 +74,29 @@ def tile_gated_adapter_bottleneck_k3_kernel(
         def bank(b):
             return psum.tile([P, N], F32, name="bank%d" % b)
 
-        def load_x_words(queue, c, g):
+        def load_x_words(c, g, lo=0, hi=CHUNK):
             rows = x_words[g].rearrange("p n t -> p (n t)")
-            queue.dma_start(out=xw[c][g][:].bitcast(I32), in_=rows[:, 4 * c * CHUNK : 4 * (c + 1) * CHUNK].bitcast(I32))
+            nc.sync.dma_start(
+                out=xw[c][g][:, lo:hi].bitcast(I32),
+                in_=rows[:, 4 * (c * CHUNK + lo) : 4 * (c * CHUNK + hi)].bitcast(I32),
+            )
 
-        def load_l_words(queue, g):
-            queue.dma_start(out=lw[g][:].bitcast(I32), in_=l_words[g].bitcast(I32))
+        def load_v_words(queue, g):
+            queue.dma_start(out=vw[g][:].bitcast(I32), in_=v_words[g].rearrange("p n t -> p (n t)").bitcast(I32))
+
+        def load_l_words(h):
+            nc.sync.dma_start(
+                out=lw[h][:].bitcast(I32), in_=l_words[2 * h : 2 * h + 2].rearrange("g p n -> p g n").bitcast(I32)
+            )
+
+        def load_d(g):
+            nc.sync.dma_start(out=d_raw[g][:], in_=d[512 * g : 512 * (g + 1), :].rearrange("(p j) n -> p j n", j=4))
+
+        def load_packed_scales(plane, rows, width):
+            for q in range(4):
+                nc.sync.dma_start(
+                    out=plane[32 * q : 32 * q + 16, :].bitcast(I32), in_=rows[:, 4 * q : 4 * q + 4, :width].bitcast(I32)
+                )
 
         def load_scale_rows(queue, plane, rows, first, width, which=range(4)):
             by_row = rows.rearrange("g (q s) n -> s q g n", s=4)
@@ -87,9 +111,11 @@ def tile_gated_adapter_bottleneck_k3_kernel(
             cols = slice(col * P, (col + 1) * P)
             x_scale = xs[c][:, g * CHUNK + col * P : g * CHUNK + (col + 1) * P]
             if which == "short":
-                rhs, rhs_scale = lw[g][:, 2 * lo : 2 * hi].bitcast(FP4X4), ls[:, g * N + lo : g * N + hi]
+                rhs, rhs_scale = lw[g // 2][:, g % 2, 2 * lo : 2 * hi].bitcast(FP4X4), ls[:, g * N + lo : g * N + hi]
             elif which == "gate":
-                rhs, rhs_scale = vw[g // 2][:, g % 2, :].bitcast(FP8X4), vs[4 * g :, :]
+                rhs, rhs_scale = vw[g][:].bitcast(FP8X4), vs[4 * g :, :]
+                if c == 0:
+                    x_scale = xp[4 * g :, cols]
             else:
                 rhs, rhs_scale = dw[g][:].bitcast(FP8X4), ds[g][:]
             nc.tensor.matmul_mx(
@@ -140,10 +166,14 @@ def tile_gated_adapter_bottleneck_k3_kernel(
             return ap.rearrange("p (u q e) -> p u q e", u=2, e=2)
 
         def store_y(t):
-            nc.sync.dma_start(out=out_0[t * P : (t + 1) * P, :], in_=y[t][:])
+            if t >= TILES - 2:
+                nc.sync.dma_start(out=out_0[t * P : (t + 1) * P, :], in_=y[t])
+            elif t % 2 == 1:
+                rows = out_0[(t - 1) * P : (t + 1) * P, :].rearrange("(a p) n -> p a n", p=P)
+                nc.sync.dma_start(out=rows, in_=y_pairs[t // 2][:])
 
         def round_y(t):
-            nc.scalar.copy(out=pair_major(y_bf[t][:]), in_=by_pairs(y[t][:]))
+            nc.scalar.copy(out=pair_major(y_bf[t][:]), in_=by_pairs(y[t]))
 
         def turn(tiles, b):
             acc = bank(b % BANKS)
@@ -154,14 +184,14 @@ def tile_gated_adapter_bottleneck_k3_kernel(
             return acc
 
         def copy_turned(tiles, acc):
-            lo, n = tiles[0] * P, len(tiles)
+            lo, n = (tiles[0] - BLOCK_TILES) * P, len(tiles)
             nc.scalar.copy(
                 out=y_turned[:, 4 * lo : 4 * (lo + n * P)].bitcast(F32).rearrange("p (a k u) -> p a k u", a=n, u=2),
                 in_=acc[:, : 2 * n * P].rearrange("p (a u k) -> p a k u", a=n, u=2),
             )
 
         def quantize_y(tiles):
-            lo, hi = tiles[0] * P, (tiles[-1] + 1) * P
+            lo, hi = (tiles[0] - BLOCK_TILES) * P, (tiles[-1] + 1 - BLOCK_TILES) * P
             nc.vector.quantize_mx(
                 out=y_codes[:, lo:hi].bitcast(FP8X4), scales=y_scales[:, lo:hi], in_=y_turned[:, 4 * lo : 4 * hi]
             )
@@ -170,7 +200,7 @@ def tile_gated_adapter_bottleneck_k3_kernel(
             rows = out_1[0].rearrange("p n t -> p (n t)")
             nc.sync.dma_start(
                 out=rows[:, 4 * first * P : 4 * (last + 1) * P].bitcast(I32),
-                in_=y_codes[:, first * P : (last + 1) * P].bitcast(I32),
+                in_=y_codes[:, (first - BLOCK_TILES) * P : (last + 1 - BLOCK_TILES) * P].bitcast(I32),
             )
 
         def store_scales(first, last, queues):
@@ -178,17 +208,47 @@ def tile_gated_adapter_bottleneck_k3_kernel(
             for q in range(4):
                 queues[q].dma_start(
                     out=out_2[0][4 * q : 4 * q + 4, cols].bitcast(I32),
-                    in_=y_scales[32 * q : 32 * q + 4, cols].bitcast(I32),
+                    in_=y_scales[32 * q : 32 * q + 4, :].bitcast(I32),
                 )
 
-        nc.vector.memset(ls[:].bitcast(I32), 0)
+        def turn_blocks(t):
+            blocks = work.tile([P, 2 * P], F32, name="blocks", align_bytes=256)
+            nc.vector.transpose(out=blocks[:], in_=y_bf[t][:].bitcast(F32))
+            joined = work.tile([P, N], BF16, name="joined", align_bytes=256)
+            nc.scalar.copy(
+                out=joined[:].bitcast(F32).rearrange("p (k u) -> p k u", u=2),
+                in_=blocks[:].rearrange("p (u k) -> p k u", u=2),
+            )
+            return joined
+
+        def quantize_blocks(t, joined):
+            cols = slice(t * P, (t + 1) * P)
+            nc.vector.quantize_mx(out=block_codes[:, cols].bitcast(FP8X4), scales=block_scales[:, cols], in_=joined[:])
+            rows = out_1[0].rearrange("p n t -> p (n t)").bitcast(I32)
+            for a in range(4):
+                nc.sync.dma_start(
+                    out=rows[:, t * P + 32 * a : t * P + 32 * (a + 1)].rearrange("(b j) i -> j b i", b=4),
+                    in_=block_codes[32 * a : 32 * (a + 1), cols].bitcast(I32).rearrange("j (b i) -> j b i", b=4),
+                )
+
+        def store_block_scales():
+            for a in range(4):
+                rows = block_scales[32 * a : 32 * a + 4, :].bitcast(I32).rearrange("r (t b w) -> r t b w", b=4, w=8)
+                for b in range(4):
+                    dest = out_2[0][4 * b : 4 * b + 4, : BLOCK_TILES * P].bitcast(I32)
+                    nc.sync.dma_start(
+                        out=dest.rearrange("r (t a w) -> r t a w", a=4, w=8)[:, :, a, :], in_=rows[:, :, b, :]
+                    )
+
+        load_v_words(nc.gpsimd, 0)
+        nc.vector.memset(vs[:].bitcast(I32), 0)
+        nc.vector.memset(xp[:].bitcast(I32), 0)
+        load_x_words(0, 0, 0, FIRST)
+        load_packed_scales(vs, v_scales, N)
+        load_packed_scales(xp, x_scales, CHUNK)
+        load_x_words(0, 0, FIRST, CHUNK)
         nc.vector.memset(zero[:], 0.0)
-        nc.vector.memset(xs[0][:].bitcast(I32), 0)
-        load_l_words(nc.sync, 0)
-        load_scale_rows(nc.sync, ls, l_scales, 0, N)
-        load_scale_rows(nc.sync, xs[0], x_scales, 0, CHUNK, (0, 1))
-        load_x_words(nc.sync, 0, 0)
-        load_scale_rows(nc.sync, xs[0], x_scales, 0, CHUNK, (2, 3))
+        nc.vector.memset(warm[:], 0.0)
         nc.vector.quantize_mx(out=zero_codes[:].bitcast(FP8X4), scales=zero_scales[:], in_=zero[:])
         idle = bank(BANKS - 1)
         for i in range(WARM_PASSES):
@@ -196,132 +256,135 @@ def tile_gated_adapter_bottleneck_k3_kernel(
                 out=idle[:, (i % 4) * P : (i % 4 + 1) * P], lhsT=zero_codes[:].bitcast(FP8X4), lhsT_scale=zero_scales[:],
                 rhs=zero_codes[:].bitcast(FP8X4), rhs_scale=zero_scales[:], start=True, stop=True,
             )
-        nc.vector.memset(vs[:].bitcast(I32), 0)
-        nc.vector.memset(xs[1][:].bitcast(I32), 0)
-        nc.vector.memset(warm[:], 0.0)
         nc.scalar.activation(out=warm[:, 1:2], in_=warm[:, 0:1], func=GELU)
+        for plane in (ls, xs[0], xs[1]):
+            nc.gpsimd.memset(plane[:].bitcast(I32), 0)
         make_identity(nc, ident[:])
         for g in range(1, PASSES):
-            load_l_words(nc.sync, g)
-            load_x_words(nc.sync, 0, g)
-        for q in range(4):
-            nc.sync.dma_start(
-                out=vs[32 * q : 32 * q + 16, :].bitcast(I32), in_=v_scales[:, 4 * q : 4 * q + 4, :].bitcast(I32)
-            )
+            load_v_words(nc.sync, g)
+            load_x_words(0, g)
+        load_scale_rows(nc.sync, ls, l_scales, 0, N)
+        load_scale_rows(nc.sync, xs[0], x_scales, 0, CHUNK)
         for h in range(2):
-            nc.sync.dma_start(
-                out=vw[h][:].bitcast(I32),
-                in_=v_words[2 * h : 2 * h + 2].rearrange("g p n t -> p g (n t)").bitcast(I32),
-            )
-        for g in range(PASSES):
-            nc.sync.dma_start(out=d_raw[g][:], in_=d[512 * g : 512 * (g + 1), :].rearrange("(p j) n -> p j n", j=4))
+            load_l_words(h)
+            load_d(2 * h)
+            load_d(2 * h + 1)
         nc.sync.dma_start(out=res[0][:], in_=r[:CHUNK, :].rearrange("(a p) n -> p a n", p=P))
         load_scale_rows(nc.sync, xs[1], x_scales, CHUNK, CHUNK)
         for g in range(PASSES):
-            load_x_words(nc.sync, 1, g)
+            load_x_words(1, g)
         nc.sync.dma_start(out=res[1][:], in_=r[CHUNK:, :].rearrange("(a p) n -> p a n", p=P))
 
-        s_acc = products("short", range(CHUNK_TILES), 0)
-        for t in range(CHUNK_TILES):
+        head = range(CHUNK_TILES)
+        g_acc = products("gate", head, 0)
+        for t in head:
             engine_copy = nc.vector.tensor_copy if t % 2 == 0 else nc.scalar.copy
-            engine_copy(out=short[t][:], in_=s_acc[t][:])
-        g_acc = products("gate", (0, 1), 6)
-        g_acc.update(products("gate", (2, 3), 0))
+            engine_copy(out=gate[t][:], in_=g_acc[t][:])
+        s_acc = products("short", head, CHUNK_TILES)
         for g in range(PASSES):
             quantize_d(g)
-        u_acc = products("down", range(4), 2)
-        for t in range(CHUNK_TILES):
-            add(short_res[t][:], short[t][:], residual(t))
-        acts = {t: gelu(u_acc[t]) for t in range(4)}
-        ring = 2
-        prods = {}
+        u_acc = products("down", (0, 1), 2 * CHUNK_TILES)
+        for t in head:
+            add(short_res[t][:], s_acc[t][:], residual(t))
+        acts = {t: gelu(u_acc[t]) for t in (0, 1)}
+        ring = 2 * CHUNK_TILES + 2
+        prods, joined = {}, {}
 
-        def finish_head(t):
-            add(y[t][:], prods[t][:], short_res[t][:])
-            store_y(t)
-            round_y(t)
+        def whole_tile(t, first_bank):
+            acts[t] = gelu(products("down", (t,), first_bank)[t])
+            g_acc.update(products("gate", (t,), first_bank + 1))
+            s_acc.update(products("short", (t,), first_bank + 2))
 
-        u_acc.update(products("down", (4,), 2))
-        g_acc.update(products("gate", (4,), 3))
-        u_acc.update(products("down", (5,), 4))
-        g_acc.update(products("gate", (5,), 5))
-        ring = 6
-        prods[0] = gated(acts[0], g_acc[0])
-        acts[4] = gelu(u_acc[4])
-        prods[1] = gated(acts[1], g_acc[1])
-        finish_head(0)
-        prods[2] = gated(acts[2], g_acc[2])
-        finish_head(1)
-        acts[5] = gelu(u_acc[5])
-        prods[3] = gated(acts[3], g_acc[3])
-        finish_head(2)
-        finish_head(3)
-        prods[4] = gated(acts[4], g_acc[4])
-        prods[5] = gated(acts[5], g_acc[5])
-
-        early_pairs = [(0, 1), (2, 3), (4, 5), (6, 7)]
-        turned = []
-
-        def finish_pairs(pairs):
-            for pair in pairs:
-                copy_turned(pair, turned.pop(0))
-
-        for t in range(CHUNK_TILES, TILES - 1):
-            act = gelu(products("down", (t,), ring)[t])
-            if t == CHUNK_TILES:
-                finish_head(4)
-                finish_head(5)
-            else:
-                round_y(t - 1)
-            if t == 9:
-                finish_pairs(early_pairs[2:])
-            prod = gated(act, products("gate", (t,), ring + 1)[t])
-            if t == 9:
-                quantize_y(early_pairs[0])
-                quantize_y(early_pairs[1])
-            if t == 10:
-                quantize_y(early_pairs[2])
-                quantize_y(early_pairs[3])
-                store_codes(0, 7)
-                store_scales(0, 7, [nc.sync] * 4)
+        def with_residual(t):
             prod_res = work.tile([P, N], F32, name="prod_res")
-            add(prod_res[:], prod[:], residual(t))
-            acc = products("short", (t,), ring + 2)[t]
-            ring += 3
-            if t == 8:
-                for pair in early_pairs:
-                    turned.append(turn(pair, ring))
-                    ring += 1
-                finish_pairs(early_pairs[:2])
-            add(y[t][:], prod_res[:], acc[:])
+            add(prod_res[:], prods[t][:], residual(t))
+            return prod_res
+
+        def finish(t, a, b):
+            add(y[t], a[:], b[:])
             store_y(t)
 
+        for t in head:
+            if t + 2 < CHUNK_TILES:
+                acts[t + 2] = gelu(products("down", (t + 2,), ring)[t + 2])
+                ring += 1
+            elif t + 2 == CHUNK_TILES:
+                whole_tile(t + 2, ring)
+                ring += 3
+            prods[t] = gated(acts[t], gate[t])
+            if t >= 1:
+                finish(t - 1, prods[t - 1], short_res[t - 1])
+                round_y(t - 1)
+            if t >= 2:
+                joined[t - 2] = turn_blocks(t - 2)
+            if t >= 3:
+                quantize_blocks(t - 3, joined[t - 3])
+
+        whole_tile(7, ring)
+        ring += 3
+        prods[6] = gated(acts[6], g_acc[6])
+        finish(5, prods[5], short_res[5])
+        round_y(5)
+        part = with_residual(6)
+        joined[4] = turn_blocks(4)
+        finish(6, part, s_acc[6])
+        round_y(6)
+        quantize_blocks(3, joined[3])
+        prods[7] = gated(acts[7], g_acc[7])
+        joined[5] = turn_blocks(5)
+        whole_tile(8, ring)
+        ring += 3
+        part = with_residual(7)
+        quantize_blocks(4, joined[4])
+        finish(7, part, s_acc[7])
+        round_y(7)
+        joined[6] = turn_blocks(6)
+        quantize_blocks(5, joined[5])
+        prods[8] = gated(acts[8], g_acc[8])
+        joined[7] = turn_blocks(7)
+        whole_tile(9, ring)
+        ring += 3
+        part = with_residual(8)
+        quantize_blocks(6, joined[6])
+        finish(8, part, s_acc[8])
+        round_y(8)
+        quantize_blocks(7, joined[7])
+        prods[9] = gated(acts[9], g_acc[9])
+        joined[8] = turn_blocks(8)
+        part = with_residual(9)
+        quantize_blocks(8, joined[8])
+        store_block_scales()
+        finish(9, part, s_acc[9])
+        parts = {}
+        for t in (10, 11):
+            acts[t] = gelu(products("down", (t,), ring)[t])
+            if t == 10:
+                round_y(9)
+            prods[t] = gated(acts[t], products("gate", (t,), ring + 1)[t])
+            parts[t] = with_residual(t)
+            ring += 2
+        finish(10, parts[10], products("short", (10,), ring)[10])
+        round_y(10)
         t = TILES - 1
-        act = gelu(products("down", (t,), ring)[t])
-        round_y(t - 1)
-        prod = gated(act, products("gate", (t,), ring + 1)[t])
-        prod_res = work.tile([P, N], F32, name="prod_res")
-        add(prod_res[:], prod[:], residual(t))
-        for i, tiles in enumerate(((8, 9), (10,))):
-            copy_turned(tiles, turn(tiles, ring + 2 + i))
-            quantize_y(tiles)
-        store_codes(8, 10)
         quarters = []
         for i in range(4):
-            acc = bank((ring + 4 + i) % BANKS)
+            acc = bank((ring + 1 + i) % BANKS)
             for g in range(PASSES):
                 mx_pass(acc, t, g, "short", i * P, (i + 1) * P)
             cols = slice(i * P, (i + 1) * P)
-            add(y_bf[t][:, cols], prod_res[:, cols], acc[:, :P])
+            add(y_bf[t][:, cols], parts[t][:, cols], acc[:, :P])
             quarters.append((cols, acc))
+        copy_turned((9, 10), turn((9, 10), ring + 5))
         for cols, acc in quarters:
-            add(y[t][:, cols], prod_res[:, cols], acc[:, :P])
+            add(y[t][:, cols], parts[t][:, cols], acc[:, :P])
         store_y(t)
-        last = bank((ring + 8) % BANKS)
+        quantize_y((9, 10))
+        store_codes(9, 10)
+        last = bank((ring + 6) % BANKS)
         words = y_bf[t][:].bitcast(F32)
         for u in range(2):
             nc.tensor.transpose(last[:, u * P : (u + 1) * P], words[:, u : 2 * P : 2], ident[:])
         copy_turned((t,), last)
         quantize_y((t,))
         store_codes(t, t)
-        store_scales(8, t, [nc.scalar, nc.scalar, nc.sync, nc.sync])
+        store_scales(BLOCK_TILES, t, [nc.scalar, nc.scalar, nc.sync, nc.sync])

@@ -20,13 +20,14 @@ GELU = mybir.ActivationFunctionType.Gelu_apprx_tanh
 P = 128
 PASSES = K // 512
 TILES = T // P
+BANKS = 8
 CHUNK_TILES = 6
 CHUNK = CHUNK_TILES * P
-BANKS = 8
+FIRST_COLUMNS = CHUNK // 2
 HALF = N // 2
+EARLY_TILES = 9
 WARM_PASSES = 16
-BLOCK_TILES = 9
-FIRST = CHUNK // 2
+WORK_BUFS = 4
 
 
 def tile_gated_adapter_bottleneck_k3_kernel(
@@ -35,7 +36,7 @@ def tile_gated_adapter_bottleneck_k3_kernel(
     nc = tc.nc
     with ExitStack() as ctx:
         keep = ctx.enter_context(tc.tile_pool(name="keep", bufs=1))
-        work = ctx.enter_context(tc.tile_pool(name="work", bufs=4))
+        work = ctx.enter_context(tc.tile_pool(name="work", bufs=WORK_BUFS))
         psum = ctx.enter_context(tc.psum_pool(name="psum", bufs=1))
         ctx.enter_context(tc.manual_schedule())
 
@@ -43,28 +44,25 @@ def tile_gated_adapter_bottleneck_k3_kernel(
             return keep.tile(shape, dtype, name=name, align_bytes=256)
 
         xw = [[kept("xw%d_%d" % (c, g), [P, CHUNK], U32) for g in range(PASSES)] for c in range(2)]
-        xp = kept("xp", [P, CHUNK], U8)
+        xs_packed = kept("xs_packed", [P, CHUNK], U8)
         xs = [kept("xs%d" % c, [P, PASSES * CHUNK], U8) for c in range(2)]
         lw = [kept("lw%d" % h, [P, 2, 2 * N], U8) for h in range(2)]
         ls = kept("ls", [P, PASSES * N], U8)
         vw = [kept("vw%d" % g, [P, N], U32) for g in range(PASSES)]
-        vs = kept("vs", [P, N], U8)
+        vs_packed = kept("vs_packed", [P, N], U8)
         d_raw = [kept("d_raw%d" % g, [P, 4, N], BF16) for g in range(PASSES)]
         d_grouped = [kept("d_grouped%d" % g, [P, N, 4], BF16) for g in range(PASSES)]
         dw = [kept("dw%d" % g, [P, N], U32) for g in range(PASSES)]
         ds = [kept("ds%d" % g, [P, N], U8) for g in range(PASSES)]
         res = [kept("res%d" % c, [P, CHUNK_TILES, N], BF16) for c in range(2)]
-        gate = [kept("gate%d" % t, [P, N], F32) for t in range(CHUNK_TILES)]
+        head_gate = [kept("head_gate%d" % t, [P, N], F32) for t in range(CHUNK_TILES)]
         short_res = [kept("short_res%d" % t, [P, N], F32) for t in range(CHUNK_TILES)]
-        y_pairs = [kept("y%d" % k, [P, 2, N], F32) for k in range(TILES // 2)]
+        y_pairs = [kept("y%d" % i, [P, 2, N], F32) for i in range(TILES // 2)]
         y = [y_pairs[t // 2][:, t % 2, :] for t in range(TILES)]
         y_bf = [kept("y_bf%d" % t, [P, N], BF16) for t in range(TILES)]
-        late = TILES - BLOCK_TILES
-        y_turned = kept("y_turned", [P, 4 * late * P], BF16)
-        y_codes = kept("y_codes", [P, late * P], U32)
-        y_scales = kept("y_scales", [P, late * P], U8)
-        block_codes = kept("block_codes", [P, BLOCK_TILES * P], U32)
-        block_scales = kept("block_scales", [P, BLOCK_TILES * P], U8)
+        y_turned = kept("y_turned", [P, 4 * T], BF16)
+        y_codes = kept("y_codes", [P, T], U32)
+        y_scales = kept("y_scales", [P, T], U8)
         ident = kept("ident", [P, P], F32)
         zero = kept("zero", [P, 4 * P], BF16)
         zero_codes = kept("zero_codes", [P, P], U32)
@@ -72,7 +70,7 @@ def tile_gated_adapter_bottleneck_k3_kernel(
         warm = kept("warm", [P, 2], F32)
 
         def bank(b):
-            return psum.tile([P, N], F32, name="bank%d" % b)
+            return psum.tile([P, N], F32, name="bank%d" % (b % BANKS))
 
         def load_x_words(c, g, lo=0, hi=CHUNK):
             rows = x_words[g].rearrange("p n t -> p (n t)")
@@ -92,16 +90,20 @@ def tile_gated_adapter_bottleneck_k3_kernel(
         def load_d(g):
             nc.sync.dma_start(out=d_raw[g][:], in_=d[512 * g : 512 * (g + 1), :].rearrange("(p j) n -> p j n", j=4))
 
+        def load_residual(c):
+            rows = r[c * CHUNK : (c + 1) * CHUNK, :]
+            nc.sync.dma_start(out=res[c][:], in_=rows.rearrange("(a p) n -> p a n", p=P))
+
         def load_packed_scales(plane, rows, width):
             for q in range(4):
                 nc.sync.dma_start(
                     out=plane[32 * q : 32 * q + 16, :].bitcast(I32), in_=rows[:, 4 * q : 4 * q + 4, :width].bitcast(I32)
                 )
 
-        def load_scale_rows(queue, plane, rows, first, width, which=range(4)):
+        def load_scales(plane, rows, first, width):
             by_row = rows.rearrange("g (q s) n -> s q g n", s=4)
-            for s in which:
-                queue.dma_start(
+            for s in range(4):
+                nc.sync.dma_start(
                     out=plane[s:P:32, :].bitcast(I32).rearrange("q (g n) -> q g n", g=PASSES),
                     in_=by_row[s][:, :, first : first + width].bitcast(I32),
                 )
@@ -113,9 +115,9 @@ def tile_gated_adapter_bottleneck_k3_kernel(
             if which == "short":
                 rhs, rhs_scale = lw[g // 2][:, g % 2, 2 * lo : 2 * hi].bitcast(FP4X4), ls[:, g * N + lo : g * N + hi]
             elif which == "gate":
-                rhs, rhs_scale = vw[g][:].bitcast(FP8X4), vs[4 * g :, :]
+                rhs, rhs_scale = vw[g][:].bitcast(FP8X4), vs_packed[4 * g :, :]
                 if c == 0:
-                    x_scale = xp[4 * g :, cols]
+                    x_scale = xs_packed[4 * g :, cols]
             else:
                 rhs, rhs_scale = dw[g][:].bitcast(FP8X4), ds[g][:]
             nc.tensor.matmul_mx(
@@ -124,11 +126,14 @@ def tile_gated_adapter_bottleneck_k3_kernel(
             )
 
         def products(which, tiles, first_bank):
-            accs = {t: bank((first_bank + i) % BANKS) for i, t in enumerate(tiles)}
+            accs = {t: bank(first_bank + i) for i, t in enumerate(tiles)}
             for g in range(PASSES):
                 for t in tiles:
                     mx_pass(accs[t], t, g, which)
             return accs
+
+        def product(which, t, b):
+            return products(which, (t,), b)[t]
 
         def quantize_d(g):
             for engine_copy, lo in ((nc.vector.tensor_copy, 0), (nc.scalar.copy, HALF)):
@@ -151,19 +156,18 @@ def tile_gated_adapter_bottleneck_k3_kernel(
             nc.scalar.activation(out=act[:], in_=acc[:], func=GELU)
             return act
 
-        def gated(act, acc):
+        def gated(act, gate):
             prod = work.tile([P, N], F32, name="prod")
-            nc.vector.tensor_tensor(out=prod[:], in0=act[:], in1=acc[:], op=MULT)
+            nc.vector.tensor_tensor(out=prod[:], in0=act[:], in1=gate[:], op=MULT)
             return prod
 
         def add(out, a, b):
             nc.vector.tensor_tensor(out=out, in0=a, in1=b, op=ADD)
 
-        def by_pairs(ap):
-            return ap.rearrange("p (q u e) -> p u q e", u=2, e=2)
-
-        def pair_major(ap):
-            return ap.rearrange("p (u q e) -> p u q e", u=2, e=2)
+        def with_residual(prod, t):
+            prod_res = work.tile([P, N], F32, name="prod_res")
+            add(prod_res[:], prod[:], residual(t))
+            return prod_res
 
         def store_y(t):
             if t >= TILES - 2:
@@ -172,26 +176,35 @@ def tile_gated_adapter_bottleneck_k3_kernel(
                 rows = out_0[(t - 1) * P : (t + 1) * P, :].rearrange("(a p) n -> p a n", p=P)
                 nc.sync.dma_start(out=rows, in_=y_pairs[t // 2][:])
 
+        def finish(t, a, b):
+            add(y[t], a[:], b[:])
+            store_y(t)
+
         def round_y(t):
-            nc.scalar.copy(out=pair_major(y_bf[t][:]), in_=by_pairs(y[t]))
+            nc.scalar.copy(
+                out=y_bf[t][:].rearrange("p (u q e) -> p u q e", u=2, e=2),
+                in_=y[t].rearrange("p (q u e) -> p u q e", u=2, e=2),
+            )
 
         def turn(tiles, b):
-            acc = bank(b % BANKS)
+            acc = bank(b)
             for i, t in enumerate(tiles):
                 words = y_bf[t][:].bitcast(F32)
                 for u in range(2):
-                    nc.tensor.transpose(acc[:, (2 * i + u) * P : (2 * i + u + 1) * P], words[:, u * P : (u + 1) * P], ident[:])
+                    nc.tensor.transpose(
+                        acc[:, (2 * i + u) * P : (2 * i + u + 1) * P], words[:, u * P : (u + 1) * P], ident[:]
+                    )
             return acc
 
         def copy_turned(tiles, acc):
-            lo, n = (tiles[0] - BLOCK_TILES) * P, len(tiles)
+            lo, count = tiles[0] * P, len(tiles)
             nc.scalar.copy(
-                out=y_turned[:, 4 * lo : 4 * (lo + n * P)].bitcast(F32).rearrange("p (a k u) -> p a k u", a=n, u=2),
-                in_=acc[:, : 2 * n * P].rearrange("p (a u k) -> p a k u", a=n, u=2),
+                out=y_turned[:, 4 * lo : 4 * (lo + count * P)].bitcast(F32).rearrange("p (a m u) -> p a m u", a=count, u=2),
+                in_=acc[:, : 2 * count * P].rearrange("p (a u m) -> p a m u", a=count, u=2),
             )
 
-        def quantize_y(tiles):
-            lo, hi = (tiles[0] - BLOCK_TILES) * P, (tiles[-1] + 1 - BLOCK_TILES) * P
+        def quantize_y(first, last):
+            lo, hi = first * P, (last + 1) * P
             nc.vector.quantize_mx(
                 out=y_codes[:, lo:hi].bitcast(FP8X4), scales=y_scales[:, lo:hi], in_=y_turned[:, 4 * lo : 4 * hi]
             )
@@ -200,7 +213,7 @@ def tile_gated_adapter_bottleneck_k3_kernel(
             rows = out_1[0].rearrange("p n t -> p (n t)")
             nc.sync.dma_start(
                 out=rows[:, 4 * first * P : 4 * (last + 1) * P].bitcast(I32),
-                in_=y_codes[:, (first - BLOCK_TILES) * P : (last + 1 - BLOCK_TILES) * P].bitcast(I32),
+                in_=y_codes[:, first * P : (last + 1) * P].bitcast(I32),
             )
 
         def store_scales(first, last, queues):
@@ -208,45 +221,17 @@ def tile_gated_adapter_bottleneck_k3_kernel(
             for q in range(4):
                 queues[q].dma_start(
                     out=out_2[0][4 * q : 4 * q + 4, cols].bitcast(I32),
-                    in_=y_scales[32 * q : 32 * q + 4, :].bitcast(I32),
+                    in_=y_scales[32 * q : 32 * q + 4, cols].bitcast(I32),
                 )
-
-        def turn_blocks(t):
-            blocks = work.tile([P, 2 * P], F32, name="blocks", align_bytes=256)
-            nc.vector.transpose(out=blocks[:], in_=y_bf[t][:].bitcast(F32))
-            joined = work.tile([P, N], BF16, name="joined", align_bytes=256)
-            nc.scalar.copy(
-                out=joined[:].bitcast(F32).rearrange("p (k u) -> p k u", u=2),
-                in_=blocks[:].rearrange("p (u k) -> p k u", u=2),
-            )
-            return joined
-
-        def quantize_blocks(t, joined):
-            cols = slice(t * P, (t + 1) * P)
-            nc.vector.quantize_mx(out=block_codes[:, cols].bitcast(FP8X4), scales=block_scales[:, cols], in_=joined[:])
-            rows = out_1[0].rearrange("p n t -> p (n t)").bitcast(I32)
-            for a in range(4):
-                nc.sync.dma_start(
-                    out=rows[:, t * P + 32 * a : t * P + 32 * (a + 1)].rearrange("(b j) i -> j b i", b=4),
-                    in_=block_codes[32 * a : 32 * (a + 1), cols].bitcast(I32).rearrange("j (b i) -> j b i", b=4),
-                )
-
-        def store_block_scales():
-            for a in range(4):
-                rows = block_scales[32 * a : 32 * a + 4, :].bitcast(I32).rearrange("r (t b w) -> r t b w", b=4, w=8)
-                for b in range(4):
-                    dest = out_2[0][4 * b : 4 * b + 4, : BLOCK_TILES * P].bitcast(I32)
-                    nc.sync.dma_start(
-                        out=dest.rearrange("r (t a w) -> r t a w", a=4, w=8)[:, :, a, :], in_=rows[:, :, b, :]
-                    )
 
         load_v_words(nc.gpsimd, 0)
-        nc.vector.memset(vs[:].bitcast(I32), 0)
-        nc.vector.memset(xp[:].bitcast(I32), 0)
-        load_x_words(0, 0, 0, FIRST)
-        load_packed_scales(vs, v_scales, N)
-        load_packed_scales(xp, x_scales, CHUNK)
-        load_x_words(0, 0, FIRST, CHUNK)
+        nc.vector.memset(vs_packed[:].bitcast(I32), 0)
+        nc.vector.memset(xs_packed[:].bitcast(I32), 0)
+        load_x_words(0, 0, 0, FIRST_COLUMNS)
+        load_packed_scales(vs_packed, v_scales, N)
+        load_packed_scales(xs_packed, x_scales, CHUNK)
+        load_x_words(0, 0, FIRST_COLUMNS, CHUNK)
+
         nc.vector.memset(zero[:], 0.0)
         nc.vector.memset(warm[:], 0.0)
         nc.vector.quantize_mx(out=zero_codes[:].bitcast(FP8X4), scales=zero_scales[:], in_=zero[:])
@@ -257,134 +242,121 @@ def tile_gated_adapter_bottleneck_k3_kernel(
                 rhs=zero_codes[:].bitcast(FP8X4), rhs_scale=zero_scales[:], start=True, stop=True,
             )
         nc.scalar.activation(out=warm[:, 1:2], in_=warm[:, 0:1], func=GELU)
+
         for plane in (ls, xs[0], xs[1]):
-            nc.gpsimd.memset(plane[:].bitcast(I32), 0)
+            nc.vector.memset(plane[:].bitcast(I32), 0)
         make_identity(nc, ident[:])
         for g in range(1, PASSES):
+            if g == PASSES - 1:
+                load_scales(ls, l_scales, 0, N)
             load_v_words(nc.sync, g)
             load_x_words(0, g)
-        load_scale_rows(nc.sync, ls, l_scales, 0, N)
-        load_scale_rows(nc.sync, xs[0], x_scales, 0, CHUNK)
-        for h in range(2):
-            load_l_words(h)
-            load_d(2 * h)
-            load_d(2 * h + 1)
-        nc.sync.dma_start(out=res[0][:], in_=r[:CHUNK, :].rearrange("(a p) n -> p a n", p=P))
-        load_scale_rows(nc.sync, xs[1], x_scales, CHUNK, CHUNK)
+        load_l_words(0)
+        load_scales(xs[0], x_scales, 0, CHUNK)
+        load_d(0)
+        load_d(1)
+        load_l_words(1)
+        load_d(2)
+        load_d(3)
+        load_residual(0)
+        load_scales(xs[1], x_scales, CHUNK, CHUNK)
         for g in range(PASSES):
             load_x_words(1, g)
-        nc.sync.dma_start(out=res[1][:], in_=r[CHUNK:, :].rearrange("(a p) n -> p a n", p=P))
+        load_residual(1)
 
         head = range(CHUNK_TILES)
-        g_acc = products("gate", head, 0)
+        gates = products("gate", head, 0)
         for t in head:
             engine_copy = nc.vector.tensor_copy if t % 2 == 0 else nc.scalar.copy
-            engine_copy(out=gate[t][:], in_=g_acc[t][:])
-        s_acc = products("short", head, CHUNK_TILES)
+            engine_copy(out=head_gate[t][:], in_=gates[t][:])
+        shorts = products("short", head, CHUNK_TILES)
         for g in range(PASSES):
             quantize_d(g)
-        u_acc = products("down", (0, 1), 2 * CHUNK_TILES)
+        downs = products("down", (0, 1), 2 * CHUNK_TILES)
         for t in head:
-            add(short_res[t][:], s_acc[t][:], residual(t))
-        acts = {t: gelu(u_acc[t]) for t in (0, 1)}
+            add(short_res[t][:], shorts[t][:], residual(t))
+        acts = {t: gelu(downs[t]) for t in (0, 1)}
         ring = 2 * CHUNK_TILES + 2
-        prods, joined = {}, {}
+        prods = {}
 
-        def whole_tile(t, first_bank):
-            acts[t] = gelu(products("down", (t,), first_bank)[t])
-            g_acc.update(products("gate", (t,), first_bank + 1))
-            s_acc.update(products("short", (t,), first_bank + 2))
+        def all_products(t, first_bank):
+            acts[t] = gelu(product("down", t, first_bank))
+            gates[t] = product("gate", t, first_bank + 1)
+            shorts[t] = product("short", t, first_bank + 2)
 
-        def with_residual(t):
-            prod_res = work.tile([P, N], F32, name="prod_res")
-            add(prod_res[:], prods[t][:], residual(t))
-            return prod_res
-
-        def finish(t, a, b):
-            add(y[t], a[:], b[:])
-            store_y(t)
+        def finish_head(t):
+            finish(t, prods[t], short_res[t])
+            round_y(t)
 
         for t in head:
             if t + 2 < CHUNK_TILES:
-                acts[t + 2] = gelu(products("down", (t + 2,), ring)[t + 2])
+                acts[t + 2] = gelu(product("down", t + 2, ring))
                 ring += 1
             elif t + 2 == CHUNK_TILES:
-                whole_tile(t + 2, ring)
+                all_products(t + 2, ring)
                 ring += 3
-            prods[t] = gated(acts[t], gate[t])
+            prods[t] = gated(acts[t], head_gate[t])
             if t >= 1:
-                finish(t - 1, prods[t - 1], short_res[t - 1])
-                round_y(t - 1)
-            if t >= 2:
-                joined[t - 2] = turn_blocks(t - 2)
-            if t >= 3:
-                quantize_blocks(t - 3, joined[t - 3])
+                finish_head(t - 1)
 
-        whole_tile(7, ring)
-        ring += 3
-        prods[6] = gated(acts[6], g_acc[6])
-        finish(5, prods[5], short_res[5])
-        round_y(5)
-        part = with_residual(6)
-        joined[4] = turn_blocks(4)
-        finish(6, part, s_acc[6])
-        round_y(6)
-        quantize_blocks(3, joined[3])
-        prods[7] = gated(acts[7], g_acc[7])
-        joined[5] = turn_blocks(5)
-        whole_tile(8, ring)
-        ring += 3
-        part = with_residual(7)
-        quantize_blocks(4, joined[4])
-        finish(7, part, s_acc[7])
-        round_y(7)
-        joined[6] = turn_blocks(6)
-        quantize_blocks(5, joined[5])
-        prods[8] = gated(acts[8], g_acc[8])
-        joined[7] = turn_blocks(7)
-        whole_tile(9, ring)
-        ring += 3
-        part = with_residual(8)
-        quantize_blocks(6, joined[6])
-        finish(8, part, s_acc[8])
-        round_y(8)
-        quantize_blocks(7, joined[7])
-        prods[9] = gated(acts[9], g_acc[9])
-        joined[8] = turn_blocks(8)
-        part = with_residual(9)
-        quantize_blocks(8, joined[8])
-        store_block_scales()
-        finish(9, part, s_acc[9])
-        parts = {}
-        for t in (10, 11):
-            acts[t] = gelu(products("down", (t,), ring)[t])
-            if t == 10:
-                round_y(9)
-            prods[t] = gated(acts[t], products("gate", (t,), ring + 1)[t])
-            parts[t] = with_residual(t)
-            ring += 2
-        finish(10, parts[10], products("short", (10,), ring)[10])
-        round_y(10)
-        t = TILES - 1
+        for t in range(CHUNK_TILES, EARLY_TILES + 1):
+            if t < EARLY_TILES:
+                all_products(t + 1, ring)
+                ring += 3
+            prods[t] = gated(acts[t], gates[t])
+            if t == CHUNK_TILES:
+                finish_head(t - 1)
+            finish(t, with_residual(prods[t], t), shorts[t])
+            if t < EARLY_TILES:
+                round_y(t)
+
+        groups = [tuple(range(t, min(t + 2, EARLY_TILES))) for t in range(0, EARLY_TILES, 2)]
+        turned = [turn(tiles, ring + i) for i, tiles in enumerate(groups)]
+        ring += len(groups)
+        copy_turned(groups[0], turned[0])
+        copy_turned(groups[1], turned[1])
+        quantize_y(0, 3)
+
+        before_last, last = TILES - 2, TILES - 1
+        act = gelu(product("down", before_last, ring))
+        copy_turned(groups[2], turned[2])
+        copy_turned(groups[3], turned[3])
+        prod = gated(act, product("gate", before_last, ring + 1))
+        quantize_y(4, 7)
+        before_last_part = with_residual(prod, before_last)
+
+        act = gelu(product("down", last, ring + 2))
+        copy_turned(groups[4], turned[4])
+        round_y(EARLY_TILES)
+        prod = gated(act, product("gate", last, ring + 3))
+        quantize_y(8, 8)
+        store_codes(0, EARLY_TILES - 1)
+        store_scales(0, EARLY_TILES - 1, [nc.sync] * 4)
+        last_part = with_residual(prod, last)
+
+        finish(before_last, before_last_part, product("short", before_last, ring + 4))
+        round_y(before_last)
+        ring += 5
+
         quarters = []
         for i in range(4):
-            acc = bank((ring + 1 + i) % BANKS)
+            acc = bank(ring + i)
             for g in range(PASSES):
-                mx_pass(acc, t, g, "short", i * P, (i + 1) * P)
+                mx_pass(acc, last, g, "short", i * P, (i + 1) * P)
             cols = slice(i * P, (i + 1) * P)
-            add(y_bf[t][:, cols], parts[t][:, cols], acc[:, :P])
+            add(y_bf[last][:, cols], last_part[:, cols], acc[:, :P])
             quarters.append((cols, acc))
-        copy_turned((9, 10), turn((9, 10), ring + 5))
+        copy_turned((EARLY_TILES, before_last), turn((EARLY_TILES, before_last), ring + 4))
         for cols, acc in quarters:
-            add(y[t][:, cols], parts[t][:, cols], acc[:, :P])
-        store_y(t)
-        quantize_y((9, 10))
-        store_codes(9, 10)
-        last = bank((ring + 6) % BANKS)
-        words = y_bf[t][:].bitcast(F32)
+            add(y[last][:, cols], last_part[:, cols], acc[:, :P])
+        store_y(last)
+        quantize_y(EARLY_TILES, before_last)
+        store_codes(EARLY_TILES, before_last)
+        acc = bank(ring + 5)
+        words = y_bf[last][:].bitcast(F32)
         for u in range(2):
-            nc.tensor.transpose(last[:, u * P : (u + 1) * P], words[:, u : 2 * P : 2], ident[:])
-        copy_turned((t,), last)
-        quantize_y((t,))
-        store_codes(t, t)
-        store_scales(BLOCK_TILES, t, [nc.scalar, nc.scalar, nc.sync, nc.sync])
+            nc.tensor.transpose(acc[:, u * P : (u + 1) * P], words[:, u : 2 * P : 2], ident[:])
+        copy_turned((last,), acc)
+        quantize_y(last, last)
+        store_codes(last, last)
+        store_scales(EARLY_TILES, last, [nc.scalar, nc.scalar, nc.sync, nc.sync])

from contextlib import ExitStack

import concourse.mybir as mybir
from concourse.masks import make_identity

T, K, N = 1536, 2048, 512
FLOPS = 3 * 2 * T * K * N

F32 = mybir.dt.float32
BF16 = mybir.dt.bfloat16
I32 = mybir.dt.int32
U32 = mybir.dt.uint32
U8 = mybir.dt.uint8
FP8X4 = mybir.dt.float8_e4m3fn_x4
FP4X4 = mybir.dt.float4_e2m1fn_x4
ADD = mybir.AluOpType.add
MULT = mybir.AluOpType.mult
GELU = mybir.ActivationFunctionType.Gelu_apprx_tanh

P = 128
PASSES = K // 512
TILES = T // P
BANKS = 8
CHUNK_TILES = 6
CHUNK = CHUNK_TILES * P
FIRST_COLUMNS = CHUNK // 2
HALF = N // 2
EARLY_TILES = 9
WARM_PASSES = 16
WORK_BUFS = 4


def tile_gated_adapter_bottleneck_k3_kernel(
    tc, x_words, x_scales, d, v_words, v_scales, l_words, l_scales, r, out_0, out_1, out_2
):
    nc = tc.nc
    with ExitStack() as ctx:
        keep = ctx.enter_context(tc.tile_pool(name="keep", bufs=1))
        work = ctx.enter_context(tc.tile_pool(name="work", bufs=WORK_BUFS))
        psum = ctx.enter_context(tc.psum_pool(name="psum", bufs=1))
        ctx.enter_context(tc.manual_schedule())

        def kept(name, shape, dtype):
            return keep.tile(shape, dtype, name=name, align_bytes=256)

        xw = [[kept("xw%d_%d" % (c, g), [P, CHUNK], U32) for g in range(PASSES)] for c in range(2)]
        xs_packed = kept("xs_packed", [P, CHUNK], U8)
        xs = [kept("xs%d" % c, [P, PASSES * CHUNK], U8) for c in range(2)]
        lw = [kept("lw%d" % h, [P, 2, 2 * N], U8) for h in range(2)]
        ls = kept("ls", [P, PASSES * N], U8)
        vw = [kept("vw%d" % g, [P, N], U32) for g in range(PASSES)]
        vs_packed = kept("vs_packed", [P, N], U8)
        d_raw = [kept("d_raw%d" % g, [P, 4, N], BF16) for g in range(PASSES)]
        d_grouped = [kept("d_grouped%d" % g, [P, N, 4], BF16) for g in range(PASSES)]
        dw = [kept("dw%d" % g, [P, N], U32) for g in range(PASSES)]
        ds = [kept("ds%d" % g, [P, N], U8) for g in range(PASSES)]
        res = [kept("res%d" % c, [P, CHUNK_TILES, N], BF16) for c in range(2)]
        head_gate = [kept("head_gate%d" % t, [P, N], F32) for t in range(CHUNK_TILES)]
        short_res = [kept("short_res%d" % t, [P, N], F32) for t in range(CHUNK_TILES)]
        y_pairs = [kept("y%d" % i, [P, 2, N], F32) for i in range(TILES // 2)]
        y = [y_pairs[t // 2][:, t % 2, :] for t in range(TILES)]
        y_bf = [kept("y_bf%d" % t, [P, N], BF16) for t in range(TILES)]
        y_turned = kept("y_turned", [P, 4 * T], BF16)
        y_codes = kept("y_codes", [P, T], U32)
        y_scales = kept("y_scales", [P, T], U8)
        ident = kept("ident", [P, P], F32)
        zero = kept("zero", [P, 4 * P], BF16)
        zero_codes = kept("zero_codes", [P, P], U32)
        zero_scales = kept("zero_scales", [P, P], U8)
        warm = kept("warm", [P, 2], F32)

        def bank(b):
            return psum.tile([P, N], F32, name="bank%d" % (b % BANKS))

        def load_x_words(c, g, lo=0, hi=CHUNK):
            rows = x_words[g].rearrange("p n t -> p (n t)")
            nc.sync.dma_start(
                out=xw[c][g][:, lo:hi].bitcast(I32),
                in_=rows[:, 4 * (c * CHUNK + lo) : 4 * (c * CHUNK + hi)].bitcast(I32),
            )

        def load_v_words(queue, g):
            queue.dma_start(out=vw[g][:].bitcast(I32), in_=v_words[g].rearrange("p n t -> p (n t)").bitcast(I32))

        def load_l_words(h):
            nc.sync.dma_start(
                out=lw[h][:].bitcast(I32), in_=l_words[2 * h : 2 * h + 2].rearrange("g p n -> p g n").bitcast(I32)
            )

        def load_d(g):
            nc.sync.dma_start(out=d_raw[g][:], in_=d[512 * g : 512 * (g + 1), :].rearrange("(p j) n -> p j n", j=4))

        def load_residual(c):
            rows = r[c * CHUNK : (c + 1) * CHUNK, :]
            nc.sync.dma_start(out=res[c][:], in_=rows.rearrange("(a p) n -> p a n", p=P))

        def load_packed_scales(plane, rows, width):
            for q in range(4):
                nc.sync.dma_start(
                    out=plane[32 * q : 32 * q + 16, :].bitcast(I32), in_=rows[:, 4 * q : 4 * q + 4, :width].bitcast(I32)
                )

        def load_scales(plane, rows, first, width):
            by_row = rows.rearrange("g (q s) n -> s q g n", s=4)
            for s in range(4):
                nc.sync.dma_start(
                    out=plane[s:P:32, :].bitcast(I32).rearrange("q (g n) -> q g n", g=PASSES),
                    in_=by_row[s][:, :, first : first + width].bitcast(I32),
                )

        def mx_pass(acc, t, g, which, lo=0, hi=N):
            c, col = divmod(t, CHUNK_TILES)
            cols = slice(col * P, (col + 1) * P)
            x_scale = xs[c][:, g * CHUNK + col * P : g * CHUNK + (col + 1) * P]
            if which == "short":
                rhs, rhs_scale = lw[g // 2][:, g % 2, 2 * lo : 2 * hi].bitcast(FP4X4), ls[:, g * N + lo : g * N + hi]
            elif which == "gate":
                rhs, rhs_scale = vw[g][:].bitcast(FP8X4), vs_packed[4 * g :, :]
                if c == 0:
                    x_scale = xs_packed[4 * g :, cols]
            else:
                rhs, rhs_scale = dw[g][:].bitcast(FP8X4), ds[g][:]
            nc.tensor.matmul_mx(
                out=acc[:, : hi - lo], lhsT=xw[c][g][:, cols].bitcast(FP8X4), lhsT_scale=x_scale,
                rhs=rhs, rhs_scale=rhs_scale, start=(g == 0), stop=(g == PASSES - 1),
            )

        def products(which, tiles, first_bank):
            accs = {t: bank(first_bank + i) for i, t in enumerate(tiles)}
            for g in range(PASSES):
                for t in tiles:
                    mx_pass(accs[t], t, g, which)
            return accs

        def product(which, t, b):
            return products(which, (t,), b)[t]

        def quantize_d(g):
            for engine_copy, lo in ((nc.vector.tensor_copy, 0), (nc.scalar.copy, HALF)):
                engine_copy(
                    out=d_grouped[g][:, lo : lo + HALF, :].rearrange("p (c i) t -> p c t i", i=4),
                    in_=d_raw[g][:, :, lo : lo + HALF].rearrange("p t (c i) -> p c t i", i=4),
                )
            flat = d_grouped[g][:].rearrange("p n t -> p (n t)")
            for lo in (0, HALF):
                nc.vector.quantize_mx(
                    out=dw[g][:, lo : lo + HALF].bitcast(FP8X4), scales=ds[g][:, lo : lo + HALF],
                    in_=flat[:, 4 * lo : 4 * (lo + HALF)],
                )

        def residual(t):
            return res[t // CHUNK_TILES][:, t % CHUNK_TILES, :]

        def gelu(acc):
            act = work.tile([P, N], F32, name="act")
            nc.scalar.activation(out=act[:], in_=acc[:], func=GELU)
            return act

        def gated(act, gate):
            prod = work.tile([P, N], F32, name="prod")
            nc.vector.tensor_tensor(out=prod[:], in0=act[:], in1=gate[:], op=MULT)
            return prod

        def add(out, a, b):
            nc.vector.tensor_tensor(out=out, in0=a, in1=b, op=ADD)

        def with_residual(prod, t):
            prod_res = work.tile([P, N], F32, name="prod_res")
            add(prod_res[:], prod[:], residual(t))
            return prod_res

        def store_y(t):
            if t >= TILES - 2:
                nc.sync.dma_start(out=out_0[t * P : (t + 1) * P, :], in_=y[t])
            elif t % 2 == 1:
                rows = out_0[(t - 1) * P : (t + 1) * P, :].rearrange("(a p) n -> p a n", p=P)
                nc.sync.dma_start(out=rows, in_=y_pairs[t // 2][:])

        def finish(t, a, b):
            add(y[t], a[:], b[:])
            store_y(t)

        def round_y(t):
            nc.scalar.copy(
                out=y_bf[t][:].rearrange("p (u q e) -> p u q e", u=2, e=2),
                in_=y[t].rearrange("p (q u e) -> p u q e", u=2, e=2),
            )

        def turn(tiles, b):
            acc = bank(b)
            for i, t in enumerate(tiles):
                words = y_bf[t][:].bitcast(F32)
                for u in range(2):
                    nc.tensor.transpose(
                        acc[:, (2 * i + u) * P : (2 * i + u + 1) * P], words[:, u * P : (u + 1) * P], ident[:]
                    )
            return acc

        def copy_turned(tiles, acc):
            lo, count = tiles[0] * P, len(tiles)
            nc.scalar.copy(
                out=y_turned[:, 4 * lo : 4 * (lo + count * P)].bitcast(F32).rearrange("p (a m u) -> p a m u", a=count, u=2),
                in_=acc[:, : 2 * count * P].rearrange("p (a u m) -> p a m u", a=count, u=2),
            )

        def quantize_y(first, last):
            lo, hi = first * P, (last + 1) * P
            nc.vector.quantize_mx(
                out=y_codes[:, lo:hi].bitcast(FP8X4), scales=y_scales[:, lo:hi], in_=y_turned[:, 4 * lo : 4 * hi]
            )

        def store_codes(first, last):
            rows = out_1[0].rearrange("p n t -> p (n t)")
            nc.sync.dma_start(
                out=rows[:, 4 * first * P : 4 * (last + 1) * P].bitcast(I32),
                in_=y_codes[:, first * P : (last + 1) * P].bitcast(I32),
            )

        def store_scales(first, last, queues):
            cols = slice(first * P, (last + 1) * P)
            for q in range(4):
                queues[q].dma_start(
                    out=out_2[0][4 * q : 4 * q + 4, cols].bitcast(I32),
                    in_=y_scales[32 * q : 32 * q + 4, cols].bitcast(I32),
                )

        load_v_words(nc.gpsimd, 0)
        nc.vector.memset(vs_packed[:].bitcast(I32), 0)
        nc.vector.memset(xs_packed[:].bitcast(I32), 0)
        load_x_words(0, 0, 0, FIRST_COLUMNS)
        load_packed_scales(vs_packed, v_scales, N)
        load_packed_scales(xs_packed, x_scales, CHUNK)
        load_x_words(0, 0, FIRST_COLUMNS, CHUNK)

        nc.vector.memset(zero[:], 0.0)
        nc.vector.memset(warm[:], 0.0)
        nc.vector.quantize_mx(out=zero_codes[:].bitcast(FP8X4), scales=zero_scales[:], in_=zero[:])
        idle = bank(BANKS - 1)
        for i in range(WARM_PASSES):
            nc.tensor.matmul_mx(
                out=idle[:, (i % 4) * P : (i % 4 + 1) * P], lhsT=zero_codes[:].bitcast(FP8X4), lhsT_scale=zero_scales[:],
                rhs=zero_codes[:].bitcast(FP8X4), rhs_scale=zero_scales[:], start=True, stop=True,
            )
        nc.scalar.activation(out=warm[:, 1:2], in_=warm[:, 0:1], func=GELU)

        for plane in (ls, xs[0], xs[1]):
            nc.vector.memset(plane[:].bitcast(I32), 0)
        make_identity(nc, ident[:])
        for g in range(1, PASSES):
            if g == PASSES - 1:
                load_scales(ls, l_scales, 0, N)
            load_v_words(nc.sync, g)
            load_x_words(0, g)
        load_l_words(0)
        load_scales(xs[0], x_scales, 0, CHUNK)
        load_d(0)
        load_d(1)
        load_l_words(1)
        load_d(2)
        load_d(3)
        load_residual(0)
        load_scales(xs[1], x_scales, CHUNK, CHUNK)
        for g in range(PASSES):
            load_x_words(1, g)
        load_residual(1)

        head = range(CHUNK_TILES)
        gates = products("gate", head, 0)
        for t in head:
            engine_copy = nc.vector.tensor_copy if t % 2 == 0 else nc.scalar.copy
            engine_copy(out=head_gate[t][:], in_=gates[t][:])
        shorts = products("short", head, CHUNK_TILES)
        for g in range(PASSES):
            quantize_d(g)
        downs = products("down", (0, 1), 2 * CHUNK_TILES)
        for t in head:
            add(short_res[t][:], shorts[t][:], residual(t))
        acts = {t: gelu(downs[t]) for t in (0, 1)}
        ring = 2 * CHUNK_TILES + 2
        prods = {}

        def all_products(t, first_bank):
            acts[t] = gelu(product("down", t, first_bank))
            gates[t] = product("gate", t, first_bank + 1)
            shorts[t] = product("short", t, first_bank + 2)

        def finish_head(t):
            finish(t, prods[t], short_res[t])
            round_y(t)

        for t in head:
            if t + 2 < CHUNK_TILES:
                acts[t + 2] = gelu(product("down", t + 2, ring))
                ring += 1
            elif t + 2 == CHUNK_TILES:
                all_products(t + 2, ring)
                ring += 3
            prods[t] = gated(acts[t], head_gate[t])
            if t >= 1:
                finish_head(t - 1)

        for t in range(CHUNK_TILES, EARLY_TILES + 1):
            if t < EARLY_TILES:
                all_products(t + 1, ring)
                ring += 3
            prods[t] = gated(acts[t], gates[t])
            if t == CHUNK_TILES:
                finish_head(t - 1)
            finish(t, with_residual(prods[t], t), shorts[t])
            if t < EARLY_TILES:
                round_y(t)

        groups = [tuple(range(t, min(t + 2, EARLY_TILES))) for t in range(0, EARLY_TILES, 2)]
        turned = [turn(tiles, ring + i) for i, tiles in enumerate(groups)]
        ring += len(groups)
        copy_turned(groups[0], turned[0])
        copy_turned(groups[1], turned[1])
        quantize_y(0, 3)

        before_last, last = TILES - 2, TILES - 1
        act = gelu(product("down", before_last, ring))
        copy_turned(groups[2], turned[2])
        copy_turned(groups[3], turned[3])
        prod = gated(act, product("gate", before_last, ring + 1))
        quantize_y(4, 7)
        before_last_part = with_residual(prod, before_last)

        act = gelu(product("down", last, ring + 2))
        copy_turned(groups[4], turned[4])
        round_y(EARLY_TILES)
        prod = gated(act, product("gate", last, ring + 3))
        quantize_y(8, 8)
        store_codes(0, EARLY_TILES - 1)
        store_scales(0, EARLY_TILES - 1, [nc.sync] * 4)
        last_part = with_residual(prod, last)

        finish(before_last, before_last_part, product("short", before_last, ring + 4))
        round_y(before_last)
        ring += 5

        quarters = []
        for i in range(4):
            acc = bank(ring + i)
            for g in range(PASSES):
                mx_pass(acc, last, g, "short", i * P, (i + 1) * P)
            cols = slice(i * P, (i + 1) * P)
            add(y_bf[last][:, cols], last_part[:, cols], acc[:, :P])
            quarters.append((cols, acc))
        copy_turned((EARLY_TILES, before_last), turn((EARLY_TILES, before_last), ring + 4))
        for cols, acc in quarters:
            add(y[last][:, cols], last_part[:, cols], acc[:, :P])
        store_y(last)
        quantize_y(EARLY_TILES, before_last)
        store_codes(EARLY_TILES, before_last)
        acc = bank(ring + 5)
        words = y_bf[last][:].bitcast(F32)
        for u in range(2):
            nc.tensor.transpose(acc[:, u * P : (u + 1) * P], words[:, u : 2 * P : 2], ident[:])
        copy_turned((last,), acc)
        quantize_y(last, last)
        store_codes(last, last)
        store_scales(EARLY_TILES, last, [nc.scalar, nc.scalar, nc.sync, nc.sync])
